import numpy as np
import ml_dtypes

BF16 = ml_dtypes.bfloat16


def bf(x):
    return np.asarray(x, np.float32).astype(BF16)


def f32(x):
    return np.asarray(x, np.float32)


def f64(x):
    return np.asarray(x).astype(np.float64)


def striped(idx):
    return np.tile(idx.reshape(-1, 16).T, (8, 1))


S, K, M, N, E, Q = 512, 128, 128, 192, 2, 96


def setup_inputs():
    return {"base": bf(np.random.standard_normal((M, S))), "x": bf(np.random.standard_normal((K, N))), "w": bf(np.random.standard_normal((E, K, M)) / np.sqrt(K)), "c": f32(0.2 + 0.8 * np.random.random_sample((1, S))), "offs": striped(np.random.permutation(S)[:N])}


def reference(base, x, w, c, offs):
    idx = offs[:16].T.reshape(-1)
    z = f64(base).copy()
    for e in range(E):
        z[:, idx[e * Q : (e + 1) * Q]] += f64(w)[e].T @ f64(x)[:, e * Q : (e + 1) * Q]
    return z * f64(c)

@@ -1,0 +1,47 @@
+import concourse.mybir as mybir
+from concourse.masks import make_identity
+
+BF16, F32, U16 = mybir.dt.bfloat16, mybir.dt.float32, mybir.dt.uint16
+P = 128
+TOKENS = 512
+LIST = 192
+EXPERTS = 2
+PIECE = LIST // EXPERTS
+PIECE_COLUMNS = PIECE // 16
+FLOPS = 2 * P * P * LIST + P * LIST + P * TOKENS
+
+
+def tile_scatter_matmul_kernel(tc, base, x, w, c, offs, out):
+    nc = tc.nc
+    with (
+        tc.tile_pool(name="held", bufs=1) as held,
+        tc.psum_pool(name="psum", bufs=1) as psum,
+    ):
+        base_tile = held.tile([P, TOKENS], BF16, name="base_tile")
+        offsets = held.tile([P, LIST // 16], U16, name="offsets")
+        w_tile = held.tile([P, EXPERTS, P], BF16, name="w_tile")
+        x_tile = held.tile([P, LIST], BF16, name="x_tile")
+        factors = held.tile([P, TOKENS], F32, name="factors")
+        ident = held.tile([P, P], BF16, name="ident")
+        result = held.tile([P, TOKENS], F32, name="result")
+        window = psum.tile([P, TOKENS], F32, name="window")
+
+        nc.sync.dma_start(base_tile[:], base)
+        nc.sync.dma_start(offsets[:], offs)
+        nc.sync.dma_start(w_tile[:], w.rearrange("e k m -> k e m"))
+        nc.sync.dma_start(x_tile[:], x)
+        nc.sync.dma_start(factors[:], c.rearrange("o t -> (o t)").partition_broadcast(P))
+        make_identity(nc, ident[:])
+
+        nc.tensor.matmul(window[:], ident[:], base_tile[:], start=True, stop=False)
+        for e in range(EXPERTS):
+            places = offsets[:, e * PIECE_COLUMNS : (e + 1) * PIECE_COLUMNS]
+            nc.tensor.matmul(
+                window[:].indirect(places),
+                w_tile[:, e, :],
+                x_tile[:, e * PIECE : (e + 1) * PIECE],
+                start=False,
+                stop=e == EXPERTS - 1,
+            )
+        nc.vector.tensor_tensor(result[:], window[:], factors[:], mybir.AluOpType.mult)
+        nc.sync.dma_start(out, result[:])

@@ -4,6 +4,7 @@ from concourse.masks import make_identity
 BF16, F32, U16 = mybir.dt.bfloat16, mybir.dt.float32, mybir.dt.uint16
 P = 128
 TOKENS = 512
+WARM_UPS = 4
 LIST = 192
 EXPERTS = 2
 PIECE = LIST // EXPERTS
@@ -24,7 +25,9 @@ def tile_scatter_matmul_kernel(tc, base, x, w, c, offs, out):
         factors = held.tile([P, TOKENS], F32, name="factors")
         ident = held.tile([P, P], BF16, name="ident")
         result = held.tile([P, TOKENS], F32, name="result")
+        zeros = held.tile([P, TOKENS], BF16, name="zeros")
         window = psum.tile([P, TOKENS], F32, name="window")
+        spare = psum.tile([P, TOKENS], F32, name="spare")
 
         nc.sync.dma_start(base_tile[:], base)
         nc.sync.dma_start(offsets[:], offs)
@@ -32,6 +35,10 @@ def tile_scatter_matmul_kernel(tc, base, x, w, c, offs, out):
         nc.sync.dma_start(x_tile[:], x)
         nc.sync.dma_start(factors[:], c.rearrange("o t -> (o t)").partition_broadcast(P))
         make_identity(nc, ident[:])
+
+        nc.vector.memset(zeros[:], 0.0)
+        for i in range(WARM_UPS):
+            nc.tensor.matmul(spare[:], zeros[:, :P], zeros[:], start=True, stop=True)
 
         nc.tensor.matmul(window[:], ident[:], base_tile[:], start=True, stop=False)
         for e in range(EXPERTS):

@@ -4,7 +4,7 @@ from concourse.masks import make_identity
 BF16, F32, U16 = mybir.dt.bfloat16, mybir.dt.float32, mybir.dt.uint16
 P = 128
 TOKENS = 512
-WARM_UPS = 4
+WARM_UPS = 3
 LIST = 192
 EXPERTS = 2
 PIECE = LIST // EXPERTS
@@ -22,23 +22,30 @@ def tile_scatter_matmul_kernel(tc, base, x, w, c, offs, out):
         offsets = held.tile([P, LIST // 16], U16, name="offsets")
         w_tile = held.tile([P, EXPERTS, P], BF16, name="w_tile")
         x_tile = held.tile([P, LIST], BF16, name="x_tile")
+        c_row = held.tile([1, TOKENS], F32, name="c_row")
+        ones = held.tile([1, P], F32, name="ones")
         factors = held.tile([P, TOKENS], F32, name="factors")
         ident = held.tile([P, P], BF16, name="ident")
         result = held.tile([P, TOKENS], F32, name="result")
         zeros = held.tile([P, TOKENS], BF16, name="zeros")
         window = psum.tile([P, TOKENS], F32, name="window")
+        spread = psum.tile([P, TOKENS], F32, name="spread")
         spare = psum.tile([P, TOKENS], F32, name="spare")
 
+        nc.scalar.dma_start(c_row[:], c)
         nc.sync.dma_start(base_tile[:], base)
         nc.sync.dma_start(offsets[:], offs)
         nc.sync.dma_start(w_tile[:], w.rearrange("e k m -> k e m"))
         nc.sync.dma_start(x_tile[:], x)
-        nc.sync.dma_start(factors[:], c.rearrange("o t -> (o t)").partition_broadcast(P))
         make_identity(nc, ident[:])
 
         nc.vector.memset(zeros[:], 0.0)
+        nc.vector.memset(ones[:], 1.0)
         for i in range(WARM_UPS):
             nc.tensor.matmul(spare[:], zeros[:, :P], zeros[:], start=True, stop=True)
+
+        nc.tensor.matmul(spread[:], ones[:], c_row[:], start=True, stop=True)
+        nc.vector.tensor_copy(factors[:], spread[:])
 
         nc.tensor.matmul(window[:], ident[:], base_tile[:], start=True, stop=False)
         for e in range(EXPERTS):

import concourse.mybir as mybir
from concourse.masks import make_identity

BF16, F32, U16 = mybir.dt.bfloat16, mybir.dt.float32, mybir.dt.uint16
P = 128
TOKENS = 512
WARM_UPS = 3
LIST = 192
EXPERTS = 2
PIECE = LIST // EXPERTS
PIECE_COLUMNS = PIECE // 16
FLOPS = 2 * P * P * LIST + P * LIST + P * TOKENS


def tile_scatter_matmul_kernel(tc, base, x, w, c, offs, out):
    nc = tc.nc
    with (
        tc.tile_pool(name="held", bufs=1) as held,
        tc.psum_pool(name="psum", bufs=1) as psum,
    ):
        base_tile = held.tile([P, TOKENS], BF16, name="base_tile")
        offsets = held.tile([P, LIST // 16], U16, name="offsets")
        w_tile = held.tile([P, EXPERTS, P], BF16, name="w_tile")
        x_tile = held.tile([P, LIST], BF16, name="x_tile")
        c_row = held.tile([1, TOKENS], F32, name="c_row")
        ones = held.tile([1, P], F32, name="ones")
        factors = held.tile([P, TOKENS], F32, name="factors")
        ident = held.tile([P, P], BF16, name="ident")
        result = held.tile([P, TOKENS], F32, name="result")
        zeros = held.tile([P, TOKENS], BF16, name="zeros")
        window = psum.tile([P, TOKENS], F32, name="window")
        spread = psum.tile([P, TOKENS], F32, name="spread")
        spare = psum.tile([P, TOKENS], F32, name="spare")

        nc.scalar.dma_start(c_row[:], c)
        nc.sync.dma_start(base_tile[:], base)
        nc.sync.dma_start(offsets[:], offs)
        nc.sync.dma_start(w_tile[:], w.rearrange("e k m -> k e m"))
        nc.sync.dma_start(x_tile[:], x)
        make_identity(nc, ident[:])

        nc.vector.memset(zeros[:], 0.0)
        nc.vector.memset(ones[:], 1.0)
        for i in range(WARM_UPS):
            nc.tensor.matmul(spare[:], zeros[:, :P], zeros[:], start=True, stop=True)

        nc.tensor.matmul(spread[:], ones[:], c_row[:], start=True, stop=True)
        nc.vector.tensor_copy(factors[:], spread[:])

        nc.tensor.matmul(window[:], ident[:], base_tile[:], start=True, stop=False)
        for e in range(EXPERTS):
            places = offsets[:, e * PIECE_COLUMNS : (e + 1) * PIECE_COLUMNS]
            nc.tensor.matmul(
                window[:].indirect(places),
                w_tile[:, e, :],
                x_tile[:, e * PIECE : (e + 1) * PIECE],
                start=False,
                stop=e == EXPERTS - 1,
            )
        nc.vector.tensor_tensor(result[:], window[:], factors[:], mybir.AluOpType.mult)
        nc.sync.dma_start(out, result[:])
